import numpy as np
import ml_dtypes


def mxq(x, axis, fmt="e4m3"):
    dtype, down = {"e4m3": (ml_dtypes.float8_e4m3fn, 7), "e5m2": (ml_dtypes.float8_e5m2, 14)}[fmt]
    v = np.moveaxis(np.asarray(x, np.float32).astype(ml_dtypes.bfloat16).astype(np.float64), axis, -1)
    blocks = v.reshape(v.shape[:-1] + (-1, 32))
    amax = np.abs(blocks).max(-1, keepdims=True)
    byte = np.maximum(np.where(amax > 0, np.frexp(amax)[1] - 1 + 127, 0) - down, 1)
    scale = np.exp2(byte - 127.0)
    codes = (blocks / scale).astype(np.float32).astype(dtype).astype(np.float64)
    return np.moveaxis((codes * scale).reshape(v.shape), -1, axis)


WIDE = False


def mx_kscale(k):
    if not WIDE:
        return np.ones(k)
    levels = np.array([10, -10, 5, -5, 0])
    if k % 512:
        return np.exp2(np.random.permutation(np.resize(levels, k // 32))).repeat(32)
    a = np.empty((k // 512, 16))
    for p in range(k // 512):
        a[p, :8] = np.random.permutation(np.resize(levels, 8))
        for g in range(8):
            far = levels[np.abs(levels - a[p, g]) >= 10]
            a[p, g + 8] = far[np.random.randint(len(far))]
    return np.exp2(a.ravel()).repeat(32)


def f64(x):
    return np.asarray(x).astype(np.float64)


def striped8(idx):
    return np.concatenate([v.reshape(-1, 16).T for v in idx]).astype(np.uint16)


def unstriped8(offs):
    return np.stack([offs[16 * g:16 * g + 16].T.reshape(-1) for g in range(8)]).astype(np.int64)


E2M1 = np.array([0.0, 0.5, 1.0, 1.5, 2.0, 3.0, 4.0, 6.0, -0.0, -0.5, -1.0, -1.5, -2.0, -3.0, -4.0, -6.0])


def pack_weight(w, fmt):
    k, n = w.shape
    w = f64(np.asarray(w, np.float32).astype(ml_dtypes.bfloat16)).reshape(k // 32, 32, n)
    amax = np.abs(w).max(1)
    if fmt == "e4m3":
        byte = np.frexp(amax)[1] - 1 + 127 - 7
    else:
        mant, ex = np.frexp(amax / 6.0)
        byte = np.where(mant > 0.5, ex, ex - 1) + 127
    byte = np.clip(np.where(amax > 0, byte, 1), 1, 254)
    scaled = (w * np.exp2(127.0 - byte)[:, None, :]).reshape(k, n).astype(np.float32)
    by_word = np.ascontiguousarray(scaled.reshape(k // 512, 128, 4, n).transpose(0, 1, 3, 2))
    if fmt == "e4m3":
        words = by_word.astype(ml_dtypes.float8_e4m3fn).view(np.uint8)
    else:
        c = by_word.astype(ml_dtypes.float4_e2m1fn).view(np.uint8) & 0xF
        words = (c[..., 0::2] | (c[..., 1::2] << 4)).reshape(k // 512, 128, 2 * n)
    return np.ascontiguousarray(words), np.ascontiguousarray(byte.astype(np.uint8).reshape(k // 512, 16, n))


def unpack_weight(words, scales, fmt):
    g, _, n = scales.shape
    words = np.ascontiguousarray(words).reshape(g, 128, n, -1)
    if fmt == "e4m3":
        vals = words.view(ml_dtypes.float8_e4m3fn).astype(np.float64)
    else:
        nib = np.empty((g, 128, n, 4), np.uint8)
        nib[..., 0::2] = words & 0xF
        nib[..., 1::2] = words >> 4
        vals = E2M1[nib]
    vals = vals * np.repeat(np.exp2(scales.astype(np.float64) - 127.0), 8, axis=1)[..., None]
    return vals.transpose(0, 1, 3, 2).reshape(g * 512, n)


def gelu(v):
    return 0.5 * v * (1.0 + np.tanh(np.sqrt(2.0 / np.pi) * (v + 0.044715 * v**3)))


K, M, T, S = 512, 512, 1024, 512


def setup_inputs():
    n = np.random.standard_normal
    s = mx_kscale(K)[:, None]
    p_w = pack_weight(n((K, M)) / np.sqrt(K) / s, "e4m3")
    return {
        "x": (n((K, S)) * s).astype(np.float32),
        "w_words": p_w[0],
        "w_scales": p_w[1],
        "b": (0.3 * n(512)).astype(np.float32),
        "wgo": np.repeat(np.random.uniform(0.5, 2.0, (8, S)), 16, axis=0).astype(np.float32),
        "offs": striped8(np.stack([np.random.permutation(T)[:S] for _ in range(8)])),
    }


def reference(x, w_words, w_scales, b, wgo, offs):
    x_ = mxq(f64(x), 0, "e4m3")
    w_ = unpack_weight(w_words, w_scales, "e4m3")
    y = w_.T @ x_
    place = unstriped8(offs)[np.arange(M) % 128 // 16]
    out = np.zeros((M, T))
    out[np.arange(M)[:, None], place] = f64(wgo)[np.arange(M) % 128] * (gelu(y + f64(b)[:, None]))
    return out

@@ -1,0 +1,93 @@
+from contextlib import ExitStack
+
+import concourse.mybir as mybir
+from concourse.masks import make_identity
+
+K, M, T, S = 512, 512, 1024, 512
+FLOPS = 2 * K * M * S
+
+F32 = mybir.dt.float32
+BF16 = mybir.dt.bfloat16
+I32 = mybir.dt.int32
+U32 = mybir.dt.uint32
+U16 = mybir.dt.uint16
+U8 = mybir.dt.uint8
+FP8X4 = mybir.dt.float8_e4m3fn_x4
+ACT = mybir.ActivationFunctionType
+MULT = mybir.AluOpType.mult
+
+P = 128
+PACK = 4
+HALF = 256
+
+
+def tile_list_hscat_gelu_kernel(tc, x, w_words, w_scales, b, wgo, offs, out):
+    nc = tc.nc
+    with ExitStack() as ctx:
+        lists = ctx.enter_context(tc.tile_pool(name="lists", bufs=1))
+        keep = ctx.enter_context(tc.tile_pool(name="keep", bufs=1))
+        psum = ctx.enter_context(tc.psum_pool(name="psum", bufs=1))
+
+        offsets = lists.tile([P, S // 16], U16, name="offsets")
+        w_codes = keep.tile([P, M], U32, name="w_codes", align_bytes=64)
+        w_plane = keep.tile([P, M], U8, name="w_plane", align_bytes=64)
+        bias = keep.tile([P, M // P], F32, name="bias")
+        bias_rows = keep.tile([P, P], F32, name="bias_rows")
+        ident = keep.tile([P, P], F32, name="ident")
+        wgo_sb = keep.tile([P, S], F32, name="wgo_sb")
+        raw = [keep.tile([P, PACK, HALF], F32, name=f"raw{h}") for h in range(2)]
+        windows = [keep.tile([P, T], F32, name=f"window{m}") for m in range(4)]
+        dummy = keep.tile([P, 1], F32, name="dummy")
+
+        x_rows = x.rearrange("(p j) w -> p j w", j=PACK)
+        nc.sync.dma_start(raw[0][:], x_rows[:, :, 0:HALF])
+        nc.gpsimd.memset(dummy[:], 0.0)
+        nc.scalar.activation(dummy[:], dummy[:], ACT.Gelu_apprx_tanh)
+        nc.gpsimd.memset(bias_rows[:], 0.0)
+        nc.gpsimd.dma_start(bias_rows[0 : M // P, :], b.rearrange("(m p) -> m p", p=P))
+        make_identity(nc, ident[:])
+        nc.vector.memset(w_plane[:].bitcast(I32), 0)
+        for q in range(4):
+            nc.sync.dma_start(
+                w_plane[32 * q : 32 * q + 4, :].bitcast(I32), w_scales[0, 4 * q : 4 * q + 4, :].bitcast(I32)
+            )
+        nc.sync.dma_start(w_codes[:].bitcast(I32), w_words[0].rearrange("p n t -> p (n t)").bitcast(I32))
+        nc.sync.dma_start(offsets[:], offs)
+        nc.sync.dma_start(wgo_sb[:], wgo)
+        nc.sync.dma_start(raw[1][:], x_rows[:, :, HALF:S])
+        for m in range(4):
+            nc.vector.memset(windows[m][:].bitcast(I32), 0)
+        bias_ps = psum.tile([P, P], F32, name="bias_ps")
+        nc.tensor.transpose(bias_ps[:], bias_rows[:], ident[:])
+        nc.scalar.copy(bias[:], bias_ps[:, 0 : M // P])
+
+        acc = [psum.tile([P, S], F32, name=f"acc{m}") for m in range(4)]
+        for h in range(2):
+            grouped = keep.tile([P, HALF, PACK], BF16, name=f"grouped{h}", align_bytes=64)
+            codes = keep.tile([P, HALF], U32, name=f"codes{h}", align_bytes=64)
+            plane = keep.tile([P, HALF], U8, name=f"plane{h}", align_bytes=64)
+            split = 168 if h == 0 else 0
+            if split:
+                nc.vector.tensor_copy(grouped[:, 0:split, :], raw[h][:, :, 0:split].rearrange("p j w -> p w j"))
+            nc.scalar.copy(grouped[:, split:HALF, :], raw[h][:, :, split:HALF].rearrange("p j w -> p w j"))
+            nc.vector.quantize_mx(
+                out=codes[:].bitcast(FP8X4), scales=plane[:], in_=grouped[:].rearrange("p w j -> p (w j)")
+            )
+            j_cols = slice(HALF * h, HALF * (h + 1))
+            for m in range(4):
+                cols = slice(P * m, P * (m + 1))
+                nc.tensor.matmul_mx(
+                    out=acc[m][:, j_cols],
+                    lhsT=w_codes[:, cols].bitcast(FP8X4),
+                    lhsT_scale=w_plane[:, cols],
+                    rhs=codes[:].bitcast(FP8X4),
+                    rhs_scale=plane[:],
+                    start=True,
+                    stop=True,
+                )
+                act = keep.tile([P, HALF], F32, name=f"act{h}{m}")
+                nc.scalar.activation(act[:], acc[m][:, j_cols], ACT.Gelu_apprx_tanh, bias=bias[:, m : m + 1])
+                place = windows[m][:].indirect(offsets[:, 16 * h : 16 * (h + 1)])
+                nc.vector.tensor_tensor(place, act[:], wgo_sb[:, j_cols], MULT)
+                if h == 1:
+                    nc.sync.dma_start(out[cols, :], windows[m][:])

@@ -1,7 +1,6 @@
 from contextlib import ExitStack
 
 import concourse.mybir as mybir
-from concourse.masks import make_identity
 
 K, M, T, S = 512, 512, 1024, 512
 FLOPS = 2 * K * M * S
@@ -32,20 +31,17 @@ def tile_list_hscat_gelu_kernel(tc, x, w_words, w_scales, b, wgo, offs, out):
         w_codes = keep.tile([P, M], U32, name="w_codes", align_bytes=64)
         w_plane = keep.tile([P, M], U8, name="w_plane", align_bytes=64)
         bias = keep.tile([P, M // P], F32, name="bias")
-        bias_rows = keep.tile([P, P], F32, name="bias_rows")
-        ident = keep.tile([P, P], F32, name="ident")
-        wgo_sb = keep.tile([P, S], F32, name="wgo_sb")
-        raw = [keep.tile([P, PACK, HALF], F32, name=f"raw{h}") for h in range(2)]
+        wgo_sb = [keep.tile([P, HALF], F32, name=f"wgo{h}") for h in range(2)]
+        raw = [keep.tile([P, PACK, HALF], F32, name=f"raw{h}", tag=f"raw{h}", align_bytes=64) for h in range(2)]
         windows = [keep.tile([P, T], F32, name=f"window{m}") for m in range(4)]
         dummy = keep.tile([P, 1], F32, name="dummy")
 
         x_rows = x.rearrange("(p j) w -> p j w", j=PACK)
-        nc.sync.dma_start(raw[0][:], x_rows[:, :, 0:HALF])
         nc.gpsimd.memset(dummy[:], 0.0)
+        with nc.allow_non_contiguous_dma(reason="one bias a partition"):
+            nc.scalar.dma_start(bias[:], b.rearrange("(m p) -> p m", p=P))
+        nc.sync.dma_start(raw[0][:], x_rows[:, :, 0:HALF])
         nc.scalar.activation(dummy[:], dummy[:], ACT.Gelu_apprx_tanh)
-        nc.gpsimd.memset(bias_rows[:], 0.0)
-        nc.gpsimd.dma_start(bias_rows[0 : M // P, :], b.rearrange("(m p) -> m p", p=P))
-        make_identity(nc, ident[:])
         nc.vector.memset(w_plane[:].bitcast(I32), 0)
         for q in range(4):
             nc.sync.dma_start(
@@ -53,41 +49,68 @@ def tile_list_hscat_gelu_kernel(tc, x, w_words, w_scales, b, wgo, offs, out):
             )
         nc.sync.dma_start(w_codes[:].bitcast(I32), w_words[0].rearrange("p n t -> p (n t)").bitcast(I32))
         nc.sync.dma_start(offsets[:], offs)
-        nc.sync.dma_start(wgo_sb[:], wgo)
+        nc.sync.dma_start(wgo_sb[0][:], wgo[:, 0:HALF])
         nc.sync.dma_start(raw[1][:], x_rows[:, :, HALF:S])
-        for m in range(4):
+        nc.sync.dma_start(wgo_sb[1][:], wgo[:, HALF:S])
+        for m in range(2):
             nc.vector.memset(windows[m][:].bitcast(I32), 0)
-        bias_ps = psum.tile([P, P], F32, name="bias_ps")
-        nc.tensor.transpose(bias_ps[:], bias_rows[:], ident[:])
-        nc.scalar.copy(bias[:], bias_ps[:, 0 : M // P])
+        for m in range(2, 4):
+            for c in range(0, T, HALF):
+                nc.gpsimd.memset(windows[m][:, c : c + HALF], 0.0)
 
         acc = [psum.tile([P, S], F32, name=f"acc{m}") for m in range(4)]
-        for h in range(2):
-            grouped = keep.tile([P, HALF, PACK], BF16, name=f"grouped{h}", align_bytes=64)
-            codes = keep.tile([P, HALF], U32, name=f"codes{h}", align_bytes=64)
-            plane = keep.tile([P, HALF], U8, name=f"plane{h}", align_bytes=64)
-            split = 168 if h == 0 else 0
+        codes = [None, None]
+        planes = [None, None]
+        acts = {}
+
+        def quantize(h, split, tag_in, tag_out):
+            grouped = keep.tile([P, HALF, PACK], BF16, name=f"grouped{h}", tag=tag_in, align_bytes=64)
+            codes[h] = keep.tile([P, HALF], U32, name=f"codes{h}", tag=tag_out, align_bytes=64)
+            planes[h] = keep.tile([P, HALF], U8, name=f"plane{h}", align_bytes=64)
             if split:
                 nc.vector.tensor_copy(grouped[:, 0:split, :], raw[h][:, :, 0:split].rearrange("p j w -> p w j"))
             nc.scalar.copy(grouped[:, split:HALF, :], raw[h][:, :, split:HALF].rearrange("p j w -> p w j"))
             nc.vector.quantize_mx(
-                out=codes[:].bitcast(FP8X4), scales=plane[:], in_=grouped[:].rearrange("p w j -> p (w j)")
+                out=codes[h][:].bitcast(FP8X4), scales=planes[h][:], in_=grouped[:].rearrange("p w j -> p (w j)")
             )
-            j_cols = slice(HALF * h, HALF * (h + 1))
-            for m in range(4):
-                cols = slice(P * m, P * (m + 1))
-                nc.tensor.matmul_mx(
-                    out=acc[m][:, j_cols],
-                    lhsT=w_codes[:, cols].bitcast(FP8X4),
-                    lhsT_scale=w_plane[:, cols],
-                    rhs=codes[:].bitcast(FP8X4),
-                    rhs_scale=plane[:],
-                    start=True,
-                    stop=True,
-                )
-                act = keep.tile([P, HALF], F32, name=f"act{h}{m}")
-                nc.scalar.activation(act[:], acc[m][:, j_cols], ACT.Gelu_apprx_tanh, bias=bias[:, m : m + 1])
-                place = windows[m][:].indirect(offsets[:, 16 * h : 16 * (h + 1)])
-                nc.vector.tensor_tensor(place, act[:], wgo_sb[:, j_cols], MULT)
-                if h == 1:
-                    nc.sync.dma_start(out[cols, :], windows[m][:])
+
+        def multiply(h, m):
+            cols = slice(P * m, P * (m + 1))
+            nc.tensor.matmul_mx(
+                out=acc[m][:, HALF * h : HALF * (h + 1)],
+                lhsT=w_codes[:, cols].bitcast(FP8X4),
+                lhsT_scale=w_plane[:, cols],
+                rhs=codes[h][:].bitcast(FP8X4),
+                rhs_scale=planes[h][:],
+                start=True,
+                stop=True,
+            )
+
+        def activate(h, m):
+            tag = {(0, 1): "late", (0, 2): "raw1"}.get((h, m), f"act{h}{m}")
+            act = keep.tile([P, HALF], F32, name=f"act{h}{m}", tag=tag, align_bytes=64)
+            nc.scalar.activation(
+                act[:], acc[m][:, HALF * h : HALF * (h + 1)], ACT.Gelu_apprx_tanh, bias=bias[:, m : m + 1]
+            )
+            acts[h, m] = act
+
+        def place(h, m):
+            nc.vector.tensor_tensor(
+                windows[m][:].indirect(offsets[:, 16 * h : 16 * (h + 1)]), acts[h, m][:], wgo_sb[h][:], MULT
+            )
+
+        quantize(0, 168, "grouped0", "share")
+        for m in range(4):
+            multiply(0, m)
+        for m in range(2):
+            activate(0, m)
+            place(0, m)
+        quantize(1, 0, "share", "late")
+        for m in range(2, 4):
+            activate(0, m)
+            place(0, m)
+        for m in range(4):
+            multiply(1, m)
+            activate(1, m)
+            place(1, m)
+            nc.sync.dma_start(out[P * m : P * (m + 1), :], windows[m][:])

@@ -38,8 +38,6 @@ def tile_list_hscat_gelu_kernel(tc, x, w_words, w_scales, b, wgo, offs, out):
 
         x_rows = x.rearrange("(p j) w -> p j w", j=PACK)
         nc.gpsimd.memset(dummy[:], 0.0)
-        with nc.allow_non_contiguous_dma(reason="one bias a partition"):
-            nc.scalar.dma_start(bias[:], b.rearrange("(m p) -> p m", p=P))
         nc.sync.dma_start(raw[0][:], x_rows[:, :, 0:HALF])
         nc.scalar.activation(dummy[:], dummy[:], ACT.Gelu_apprx_tanh)
         nc.vector.memset(w_plane[:].bitcast(I32), 0)
@@ -48,13 +46,15 @@ def tile_list_hscat_gelu_kernel(tc, x, w_words, w_scales, b, wgo, offs, out):
                 w_plane[32 * q : 32 * q + 4, :].bitcast(I32), w_scales[0, 4 * q : 4 * q + 4, :].bitcast(I32)
             )
         nc.sync.dma_start(w_codes[:].bitcast(I32), w_words[0].rearrange("p n t -> p (n t)").bitcast(I32))
+        with nc.allow_non_contiguous_dma(reason="one bias a partition"):
+            nc.sync.dma_start(bias[:], b.rearrange("(m p) -> p m", p=P))
         nc.sync.dma_start(offsets[:], offs)
         nc.sync.dma_start(wgo_sb[0][:], wgo[:, 0:HALF])
         nc.sync.dma_start(raw[1][:], x_rows[:, :, HALF:S])
         nc.sync.dma_start(wgo_sb[1][:], wgo[:, HALF:S])
-        for m in range(2):
+        for m in range(3):
             nc.vector.memset(windows[m][:].bitcast(I32), 0)
-        for m in range(2, 4):
+        for m in range(3, 4):
             for c in range(0, T, HALF):
                 nc.gpsimd.memset(windows[m][:, c : c + HALF], 0.0)
 

from contextlib import ExitStack

import concourse.mybir as mybir

K, M, T, S = 512, 512, 1024, 512
FLOPS = 2 * K * M * S

F32 = mybir.dt.float32
BF16 = mybir.dt.bfloat16
I32 = mybir.dt.int32
U32 = mybir.dt.uint32
U16 = mybir.dt.uint16
U8 = mybir.dt.uint8
FP8X4 = mybir.dt.float8_e4m3fn_x4
ACT = mybir.ActivationFunctionType
MULT = mybir.AluOpType.mult

P = 128
PACK = 4
HALF = 256


def tile_list_hscat_gelu_kernel(tc, x, w_words, w_scales, b, wgo, offs, out):
    nc = tc.nc
    with ExitStack() as ctx:
        lists = ctx.enter_context(tc.tile_pool(name="lists", bufs=1))
        keep = ctx.enter_context(tc.tile_pool(name="keep", bufs=1))
        psum = ctx.enter_context(tc.psum_pool(name="psum", bufs=1))

        offsets = lists.tile([P, S // 16], U16, name="offsets")
        w_codes = keep.tile([P, M], U32, name="w_codes", align_bytes=64)
        w_plane = keep.tile([P, M], U8, name="w_plane", align_bytes=64)
        bias = keep.tile([P, M // P], F32, name="bias")
        wgo_sb = [keep.tile([P, HALF], F32, name=f"wgo{h}") for h in range(2)]
        raw = [keep.tile([P, PACK, HALF], F32, name=f"raw{h}", tag=f"raw{h}", align_bytes=64) for h in range(2)]
        windows = [keep.tile([P, T], F32, name=f"window{m}") for m in range(4)]
        dummy = keep.tile([P, 1], F32, name="dummy")

        x_rows = x.rearrange("(p j) w -> p j w", j=PACK)
        nc.gpsimd.memset(dummy[:], 0.0)
        nc.sync.dma_start(raw[0][:], x_rows[:, :, 0:HALF])
        nc.scalar.activation(dummy[:], dummy[:], ACT.Gelu_apprx_tanh)
        nc.vector.memset(w_plane[:].bitcast(I32), 0)
        for q in range(4):
            nc.sync.dma_start(
                w_plane[32 * q : 32 * q + 4, :].bitcast(I32), w_scales[0, 4 * q : 4 * q + 4, :].bitcast(I32)
            )
        nc.sync.dma_start(w_codes[:].bitcast(I32), w_words[0].rearrange("p n t -> p (n t)").bitcast(I32))
        with nc.allow_non_contiguous_dma(reason="one bias a partition"):
            nc.sync.dma_start(bias[:], b.rearrange("(m p) -> p m", p=P))
        nc.sync.dma_start(offsets[:], offs)
        nc.sync.dma_start(wgo_sb[0][:], wgo[:, 0:HALF])
        nc.sync.dma_start(raw[1][:], x_rows[:, :, HALF:S])
        nc.sync.dma_start(wgo_sb[1][:], wgo[:, HALF:S])
        for m in range(3):
            nc.vector.memset(windows[m][:].bitcast(I32), 0)
        for m in range(3, 4):
            for c in range(0, T, HALF):
                nc.gpsimd.memset(windows[m][:, c : c + HALF], 0.0)

        acc = [psum.tile([P, S], F32, name=f"acc{m}") for m in range(4)]
        codes = [None, None]
        planes = [None, None]
        acts = {}

        def quantize(h, split, tag_in, tag_out):
            grouped = keep.tile([P, HALF, PACK], BF16, name=f"grouped{h}", tag=tag_in, align_bytes=64)
            codes[h] = keep.tile([P, HALF], U32, name=f"codes{h}", tag=tag_out, align_bytes=64)
            planes[h] = keep.tile([P, HALF], U8, name=f"plane{h}", align_bytes=64)
            if split:
                nc.vector.tensor_copy(grouped[:, 0:split, :], raw[h][:, :, 0:split].rearrange("p j w -> p w j"))
            nc.scalar.copy(grouped[:, split:HALF, :], raw[h][:, :, split:HALF].rearrange("p j w -> p w j"))
            nc.vector.quantize_mx(
                out=codes[h][:].bitcast(FP8X4), scales=planes[h][:], in_=grouped[:].rearrange("p w j -> p (w j)")
            )

        def multiply(h, m):
            cols = slice(P * m, P * (m + 1))
            nc.tensor.matmul_mx(
                out=acc[m][:, HALF * h : HALF * (h + 1)],
                lhsT=w_codes[:, cols].bitcast(FP8X4),
                lhsT_scale=w_plane[:, cols],
                rhs=codes[h][:].bitcast(FP8X4),
                rhs_scale=planes[h][:],
                start=True,
                stop=True,
            )

        def activate(h, m):
            tag = {(0, 1): "late", (0, 2): "raw1"}.get((h, m), f"act{h}{m}")
            act = keep.tile([P, HALF], F32, name=f"act{h}{m}", tag=tag, align_bytes=64)
            nc.scalar.activation(
                act[:], acc[m][:, HALF * h : HALF * (h + 1)], ACT.Gelu_apprx_tanh, bias=bias[:, m : m + 1]
            )
            acts[h, m] = act

        def place(h, m):
            nc.vector.tensor_tensor(
                windows[m][:].indirect(offsets[:, 16 * h : 16 * (h + 1)]), acts[h, m][:], wgo_sb[h][:], MULT
            )

        quantize(0, 168, "grouped0", "share")
        for m in range(4):
            multiply(0, m)
        for m in range(2):
            activate(0, m)
            place(0, m)
        quantize(1, 0, "share", "late")
        for m in range(2, 4):
            activate(0, m)
            place(0, m)
        for m in range(4):
            multiply(1, m)
            activate(1, m)
            place(1, m)
            nc.sync.dma_start(out[P * m : P * (m + 1), :], windows[m][:])
